import numpy as np
import ml_dtypes


def mxq(x, axis, fmt="e4m3"):
    dtype, down = {"e4m3": (ml_dtypes.float8_e4m3fn, 7), "e5m2": (ml_dtypes.float8_e5m2, 14)}[fmt]
    v = np.moveaxis(np.asarray(x, np.float32).astype(ml_dtypes.bfloat16).astype(np.float64), axis, -1)
    blocks = v.reshape(v.shape[:-1] + (-1, 32))
    amax = np.abs(blocks).max(-1, keepdims=True)
    byte = np.maximum(np.where(amax > 0, np.frexp(amax)[1] - 1 + 127, 0) - down, 1)
    scale = np.exp2(byte - 127.0)
    codes = (blocks / scale).astype(np.float32).astype(dtype).astype(np.float64)
    return np.moveaxis((codes * scale).reshape(v.shape), -1, axis)


WIDE = False


def mx_kscale(k):
    if not WIDE:
        return np.ones(k)
    levels = np.array([10, -10, 5, -5, 0])
    if k % 512:
        return np.exp2(np.random.permutation(np.resize(levels, k // 32))).repeat(32)
    a = np.empty((k // 512, 16))
    for p in range(k // 512):
        a[p, :8] = np.random.permutation(np.resize(levels, 8))
        for g in range(8):
            far = levels[np.abs(levels - a[p, g]) >= 10]
            a[p, g + 8] = far[np.random.randint(len(far))]
    return np.exp2(a.ravel()).repeat(32)


def f64(x):
    return np.asarray(x).astype(np.float64)


def striped(idx):
    return np.tile(np.asarray(idx).reshape(-1, 16).T, (8, 1)).astype(np.uint16)


def unstriped(offs):
    return offs[:16].T.reshape(-1).astype(np.int64)


E2M1 = np.array([0.0, 0.5, 1.0, 1.5, 2.0, 3.0, 4.0, 6.0, -0.0, -0.5, -1.0, -1.5, -2.0, -3.0, -4.0, -6.0])


def pack_weight(w, fmt):
    k, n = w.shape
    w = f64(np.asarray(w, np.float32).astype(ml_dtypes.bfloat16)).reshape(k // 32, 32, n)
    amax = np.abs(w).max(1)
    if fmt == "e4m3":
        byte = np.frexp(amax)[1] - 1 + 127 - 7
    else:
        mant, ex = np.frexp(amax / 6.0)
        byte = np.where(mant > 0.5, ex, ex - 1) + 127
    byte = np.clip(np.where(amax > 0, byte, 1), 1, 254)
    scaled = (w * np.exp2(127.0 - byte)[:, None, :]).reshape(k, n).astype(np.float32)
    by_word = np.ascontiguousarray(scaled.reshape(k // 512, 128, 4, n).transpose(0, 1, 3, 2))
    if fmt == "e4m3":
        words = by_word.astype(ml_dtypes.float8_e4m3fn).view(np.uint8)
    else:
        c = by_word.astype(ml_dtypes.float4_e2m1fn).view(np.uint8) & 0xF
        words = (c[..., 0::2] | (c[..., 1::2] << 4)).reshape(k // 512, 128, 2 * n)
    return np.ascontiguousarray(words), np.ascontiguousarray(byte.astype(np.uint8).reshape(k // 512, 16, n))


def unpack_weight(words, scales, fmt):
    g, _, n = scales.shape
    words = np.ascontiguousarray(words).reshape(g, 128, n, -1)
    if fmt == "e4m3":
        vals = words.view(ml_dtypes.float8_e4m3fn).astype(np.float64)
    else:
        nib = np.empty((g, 128, n, 4), np.uint8)
        nib[..., 0::2] = words & 0xF
        nib[..., 1::2] = words >> 4
        vals = E2M1[nib]
    vals = vals * np.repeat(np.exp2(scales.astype(np.float64) - 127.0), 8, axis=1)[..., None]
    return vals.transpose(0, 1, 3, 2).reshape(g * 512, n)


def sigmoid(v):
    return 1.0 / (1.0 + np.exp(-v))


D, T, I, Q, E = 512, 2048, 512, 128, 512


def setup_inputs():
    n = np.random.standard_normal
    idx = np.random.permutation(T)[:I]
    idx4 = np.random.permutation(I)[:I]
    fd = mx_kscale(D)
    fi = mx_kscale(I)
    ti = np.ones(T)
    ti[idx] = fi
    keysp = pack_weight(n((D, T)) / fd[:, None], "e4m3")
    return {
        "query": (n((D, Q)) * 1.2 / np.sqrt(D) * fd[:, None]).astype(np.float32),
        "keys_words": keysp[0],
        "keys_scales": keysp[1],
        "guess": np.tile(np.random.uniform(0.05, 0.3, T), (128, 1)).astype(np.float32),
        "steep": np.tile(np.random.uniform(1.0, 3.0, T), (128, 1)).astype(np.float32),
        "thr": np.tile(np.random.uniform(-0.5, 1.0, T), (128, 1)).astype(np.float32),
        "lam": (np.random.uniform(0.6, 1.5, (Q, 1))).astype(np.float32),
        "pull": (np.random.uniform(0.4, 1.2, (Q, 1))).astype(np.float32),
        "os": (np.random.uniform(4.0, 16.0, (1, I)) * fi).astype(np.float32),
        "vals": (n((E, T)) / ti).astype(np.float32),
        "offs": striped(idx),
        "offs4": striped(idx4),
    }


def reference(query, keys_words, keys_scales, guess, steep, thr, lam, pull, os, vals, offs, offs4):
    idx = unstriped(offs)
    idx4 = unstriped(offs4)
    keysu = unpack_weight(keys_words, keys_scales, "e4m3")
    queryq = mxq(f64(query), 0, "e4m3")
    keysidxg = keysu[:, idx]
    a = queryq.T @ keysidxg
    sg = sigmoid((a - f64(thr)[:1][:, idx]) * f64(steep)[:1][:, idx])
    s = np.log(sg * (1.0 - f64(guess)[:1][:, idx]) + f64(guess)[:1][:, idx]) * f64(lam)
    p = np.exp(s - np.max(s, axis=1, keepdims=True))
    r = p / np.sum(p, axis=1, keepdims=True)
    w = r + r[:, idx4] * f64(pull)
    wo1 = w * f64(os)
    wt1 = wo1.T
    vt1 = f64(vals)[:, idx].T
    wt1q = mxq(wt1, 0, "e4m3")
    vt1q = mxq(vt1, 0, "e4m3")
    o = wt1q.T @ vt1q
    return o

@@ -1,0 +1,225 @@
+from contextlib import ExitStack
+
+import concourse.mybir as mybir
+from concourse.masks import make_identity
+
+D, T, I, Q, E = 512, 2048, 512, 128, 512
+FLOPS = 2 * Q * I * D + 2 * Q * I * E
+BYTES = D * Q * 4 + D * T + 16 * T + 3 * T * 4 + 2 * Q * 4 + I * 4 + E * T * 4 + 2 * 128 * 32 * 2 + Q * E * 4
+
+F32 = mybir.dt.float32
+BF16 = mybir.dt.bfloat16
+I32 = mybir.dt.int32
+U32 = mybir.dt.uint32
+U16 = mybir.dt.uint16
+U8 = mybir.dt.uint8
+FP8X4 = mybir.dt.float8_e4m3fn_x4
+ALU = mybir.AluOpType
+ACT = mybir.ActivationFunctionType
+
+P = 128
+LIVE = P - 1
+R_WINDOW = 704
+
+
+def tile_attend_answerodds_followed_read_kernel(
+    tc, query, keys_words, keys_scales, guess, steep, thr, lam, pull, slot_factor, vals, offs, offs4, out
+):
+    nc = tc.nc
+    with ExitStack() as ctx:
+        lists = ctx.enter_context(tc.tile_pool(name="lists", bufs=1))
+        sb = ctx.enter_context(tc.tile_pool(name="sb", bufs=1))
+        late = ctx.enter_context(tc.tile_pool(name="late", bufs=1))
+        ps = ctx.enter_context(tc.psum_pool(name="ps", bufs=1))
+
+        def bank(tag, name):
+            return ps.tile([P, 4, P], F32, tag=tag, name=name)
+
+        offs_sb = lists.tile([P, I // 16], U16, name="offs_sb")
+        offs4_sb = lists.tile([P, I // 16], U16, name="offs4_sb")
+
+        warm = sb.tile([P, 8], F32, name="warm")
+        warm_out = sb.tile([P, 8], F32, name="warm_out")
+        nc.vector.memset(warm[:], 0.0)
+        ksc = sb.tile([P, T], U8, name="ksc", align_bytes=64)
+        nc.vector.memset(ksc[:].bitcast(I32), 0)
+        thr_w = sb.tile([P, T], F32, name="thr_w", tag="row_a")
+        steep_w = sb.tile([P, T], F32, name="steep_w", tag="row_b")
+        nc.vector.memset(thr_w[0:LIVE, :], 0.0)
+        nc.vector.memset(steep_w[0:LIVE, :], 0.0)
+        guess_w = sb.tile([P, T], F32, name="guess_w")
+        nc.vector.memset(guess_w[0:LIVE, 0:64], 0.0)
+
+        nc.sync.dma_start(offs_sb[:], offs)
+        nc.sync.dma_start(thr_w[LIVE:P, :], thr[0:1, :])
+        nc.sync.dma_start(steep_w[LIVE:P, :], steep[0:1, :])
+        nc.scalar.activation(warm_out[:], warm[:], ACT.Sigmoid)
+        kw = sb.tile([P, T], I32, name="kw", align_bytes=64)
+        nc.sync.dma_start(kw[:], keys_words[0].rearrange("p n t -> p (n t)").bitcast(I32))
+        sc_rows = keys_scales[0].rearrange("(g r) n -> r g n", r=4)
+        for r in range(4):
+            nc.sync.dma_start(ksc[r:P:32, :].bitcast(I32), sc_rows[r].bitcast(I32))
+        q_raw = sb.tile([P, 4, Q], F32, name="q_raw", tag="q")
+        nc.sync.dma_start(q_raw[:], query.rearrange("(p j) q -> p j q", j=4))
+        nc.sync.dma_start(guess_w[LIVE:P, :], guess[0:1, :])
+        v_w = [sb.tile([P, T], F32, name="v_w%d" % j, tag="v%d" % j, align_bytes=64) for j in range(3)]
+        v_w.append(late.tile([P, T], F32, name="v_w3", offset=0, align_bytes=64))
+        nc.sync.dma_start(v_w[0][:], vals[0:P, :])
+        lam_sb = sb.tile([P, 1], F32, name="lam_sb")
+        nc.sync.dma_start(lam_sb[:], lam)
+        nc.sync.dma_start(v_w[1][:], vals[P : 2 * P, :])
+
+        ident = sb.tile([P, P], F32, name="ident")
+        make_identity(nc, ident[:])
+        r_w = sb.tile([P, R_WINDOW], F32, name="r_w")
+        nc.gpsimd.memset(r_w[:, I:R_WINDOW], 0.0)
+        nc.gpsimd.memset(guess_w[0:LIVE, 32:T], 0.0)
+
+        def turn4(dst, src):
+            for t in range(4):
+                nc.tensor.transpose(dst[:, t, :], src[:, t * P : (t + 1) * P], ident[:])
+
+        thr_g = sb.tile([P, I], F32, name="thr_g")
+        nc.vector.tensor_copy(thr_g[:], thr_w[:].indirect(offs_sb[:]))
+        steep_g = sb.tile([P, I], F32, name="steep_g")
+        nc.vector.tensor_copy(steep_g[:], steep_w[:].indirect(offs_sb[:]))
+        thr_t = bank("b0", "thr_t")
+        turn4(thr_t, thr_g)
+        steep_t = bank("b1", "steep_t")
+        turn4(steep_t, steep_g)
+
+        nc.sync.dma_start(offs4_sb[:], offs4)
+        pull_sb = sb.tile([P, 1], F32, name="pull_sb")
+        nc.sync.dma_start(pull_sb[:], pull)
+        os_sb = sb.tile([P, 4], F32, name="os_sb")
+        nc.sync.dma_start(os_sb[:], slot_factor.rearrange("o (p t) -> (o p) t", t=4))
+        for j in range(2, 4):
+            nc.sync.dma_start(v_w[j][:], vals[j * P : (j + 1) * P, :])
+
+        q_bf = sb.tile([P, Q, 4], BF16, name="q_bf", align_bytes=64)
+        nc.scalar.copy(q_bf[:], q_raw[:].rearrange("p j q -> p q j"))
+        steep_pair = sb.tile([P, 8], F32, name="steep_pair", tag="q")
+        steep_c = steep_pair[:, 0:4]
+        nsteep_c = steep_pair[:, 4:8]
+        bias_c = sb.tile([P, 4], F32, name="bias_c")
+        nc.scalar.activation(steep_c, steep_t[:, :, LIVE], ACT.Copy)
+        nc.scalar.activation(nsteep_c, steep_t[:, :, LIVE], ACT.Copy, scale=-1.0)
+        for t in range(4):
+            nc.scalar.activation(bias_c[:, t : t + 1], thr_t[:, t, LIVE:P], ACT.Copy, scale=nsteep_c[:, t : t + 1])
+
+        q_codes = sb.tile([P, Q], U32, name="q_codes", align_bytes=64)
+        q_scales = sb.tile([P, Q], U8, name="q_scales", align_bytes=64)
+
+        kw_g = sb.tile([P, I], U32, name="kw_g", align_bytes=64)
+        ksc_g = sb.tile([P, I], U8, name="ksc_g", align_bytes=64)
+        nc.vector.tensor_copy(kw_g[:], kw[:].bitcast(U32).indirect(offs_sb[:]))
+        nc.vector.quantize_mx(out=q_codes[:].bitcast(FP8X4), scales=q_scales[:], in_=q_bf[:].rearrange("p q j -> p (q j)"))
+        nc.vector.tensor_copy(ksc_g[:], ksc[:].indirect(offs_sb[:]))
+
+        a_t = bank("b3", "a_t")
+        for t in range(4):
+            cols = slice(t * P, (t + 1) * P)
+            nc.tensor.matmul_mx(
+                out=a_t[:, t, :],
+                lhsT=kw_g[:, cols].bitcast(FP8X4),
+                lhsT_scale=ksc_g[:, cols],
+                rhs=q_codes[:].bitcast(FP8X4),
+                rhs_scale=q_scales[:],
+                start=True,
+                stop=True,
+            )
+        sg = sb.tile([P, 4, P], F32, name="sg")
+        for t in range(4):
+            nc.scalar.activation(sg[:, t, :], a_t[:, t, :], ACT.Sigmoid, bias=bias_c[:, t : t + 1], scale=steep_c[:, t : t + 1])
+
+        guess_g = sb.tile([P, I], F32, name="guess_g")
+        nc.vector.tensor_copy(guess_g[:], guess_w[:].indirect(offs_sb[:]))
+        guess_t = bank("b2", "guess_t")
+        turn4(guess_t, guess_g)
+
+        def turn_values(j, v_t):
+            v_g = sb.tile([P, I], BF16, name="v_g%d" % j)
+            nc.vector.tensor_copy(v_g[:], v_w[j][:].indirect(offs_sb[:]))
+            words = v_g[:].bitcast(F32)
+            for u in range(2):
+                nc.tensor.transpose(v_t[:, u, :], words[:, u : 2 * P : 2], ident[:])
+
+        v_t01 = ps.tile([P, 2, 2, P], F32, tag="bv0", name="v_t01")
+        turn_values(0, v_t01[:, 0, :, :])
+        guess_rest = sb.tile([P, 8], F32, name="guess_rest", tag="v0", align_bytes=64)
+        guess_c = guess_rest[:, 0:4]
+        rest_c = guess_rest[:, 4:8]
+        nc.vector.tensor_copy(guess_c, guess_t[:, :, LIVE])
+        nc.vector.tensor_scalar(rest_c, guess_t[:, :, LIVE], -1.0, 1.0, ALU.mult, ALU.add)
+        nlam = sb.tile([P, 1], F32, name="nlam")
+        nc.gpsimd.tensor_scalar(nlam[:], lam_sb[:], -1.0, 0.0, ALU.mult, ALU.add)
+
+        ln_t = sb.tile([P, I], F32, name="ln_t")
+        for t in range(4):
+            nc.scalar.activation(ln_t[:, t * P : (t + 1) * P], sg[:, t, :], ACT.Ln, bias=guess_c[:, t : t + 1], scale=rest_c[:, t : t + 1])
+        turn_values(1, v_t01[:, 1, :, :])
+        ln_q = bank("b0", "ln_q")
+        turn4(ln_q, ln_t)
+        neg_s = sb.tile([P, I], F32, name="neg_s", tag="v1", align_bytes=64)
+        neg_max = sb.tile([P, 1], F32, name="neg_max")
+        nc.vector.tensor_scalar(neg_s[:], ln_q[:].rearrange("p t s -> p (t s)"), nlam[:], None, ALU.mult, ALU.min, accum_out=neg_max[:])
+        v_t2 = ps.tile([P, 2, P], F32, tag="bv1", name="v_t2")
+        turn_values(2, v_t2)
+        p_sb = sb.tile([P, I], F32, name="p_sb")
+        row_sum = sb.tile([P, 1], F32, name="row_sum")
+        nc.scalar.activation(p_sb[:], neg_s[:], ACT.Exp, bias=neg_max[:], scale=-1.0, accum_out=row_sum[:])
+        v_bf01 = sb.tile([P, 2 * P, 4], BF16, name="v_bf01", tag="v1", align_bytes=64)
+        v_bf23 = sb.tile([P, 2 * P, 4], BF16, name="v_bf23", align_bytes=64)
+        words01 = v_bf01[:].rearrange("p e t -> p (e t)").bitcast(F32)
+        words23 = v_bf23[:].rearrange("p e t -> p (e t)").bitcast(F32)
+        nc.scalar.copy(words01.rearrange("p (j e u) -> p j e u", j=2, u=2), v_t01[:].rearrange("p j u e -> p j e u"))
+        nc.scalar.copy(words23[:, 0 : 2 * P].rearrange("p (e u) -> p e u", u=2), v_t2[:].rearrange("p u e -> p e u"))
+        inv_sum = sb.tile([P, 1], F32, name="inv_sum", tag="v2", align_bytes=64)
+        nc.vector.reciprocal(inv_sum[:], row_sum[:])
+        nc.vector.tensor_scalar(r_w[:, 0:I], p_sb[:], inv_sum[:], None, ALU.mult)
+        r_g = sb.tile([P, I], F32, name="r_g")
+        nc.vector.tensor_copy(r_g[:], r_w[:].indirect(offs4_sb[:]))
+        w_d = sb.tile([P, I], F32, name="w_d")
+        nc.vector.scalar_tensor_tensor(
+            w_d[:].rearrange("p (t s) -> p s t", t=4),
+            r_g[:].rearrange("p (s t) -> p s t", t=4),
+            pull_sb[:],
+            r_w[:, 0:I].rearrange("p (s t) -> p s t", t=4),
+            ALU.mult,
+            ALU.add,
+        )
+        w_t = bank("b1", "w_t")
+        turn4(w_t, w_d)
+        v_t3 = ps.tile([P, 2, P], F32, tag="b0", name="v_t3")
+        turn_values(3, v_t3)
+        nc.scalar.copy(words23[:, 2 * P : 4 * P].rearrange("p (e u) -> p e u", u=2), v_t3[:].rearrange("p u e -> p e u"))
+        w_bf = late.tile([P, Q, 4], BF16, name="w_bf", offset=0, align_bytes=64)
+        nc.vector.tensor_tensor(w_bf[:], w_t[:].rearrange("p t q -> p q t"), os_sb[:].unsqueeze(1).to_broadcast([P, Q, 4]), ALU.mult)
+        half = E // 2
+        v_codes = [late.tile([P, half], U32, name="v_codes%d" % h, offset=1024 * (1 + h), align_bytes=64) for h in range(2)]
+        v_scales = [sb.tile([P, half], U8, name="v_scales%d" % h, align_bytes=64) for h in range(2)]
+        nc.vector.quantize_mx(out=v_codes[0][:].bitcast(FP8X4), scales=v_scales[0][:], in_=v_bf01[:].rearrange("p e t -> p (e t)"))
+        w_codes = sb.tile([P, Q], U32, name="w_codes", align_bytes=64)
+        w_scales = sb.tile([P, Q], U8, name="w_scales", align_bytes=64)
+        nc.vector.quantize_mx(out=w_codes[:].bitcast(FP8X4), scales=w_scales[:], in_=w_bf[:].rearrange("p q t -> p (q t)"))
+        nc.vector.quantize_mx(out=v_codes[1][:].bitcast(FP8X4), scales=v_scales[1][:], in_=v_bf23[:].rearrange("p e t -> p (e t)"))
+
+        for h in range(2):
+            cols = slice(h * half, (h + 1) * half)
+            o_ps = ps.tile([P, half], F32, tag="b%d" % (2 + h), name="o_ps%d" % h)
+            nc.tensor.matmul_mx(
+                out=o_ps[:],
+                lhsT=w_codes[:].bitcast(FP8X4),
+                lhsT_scale=w_scales[:],
+                rhs=v_codes[h][:].bitcast(FP8X4),
+                rhs_scale=v_scales[h][:],
+                start=True,
+                stop=True,
+            )
+            o_sb = sb.tile([P, half], F32, name="o_sb%d" % h)
+            if h == 1:
+                nc.vector.tensor_copy(o_sb[:], o_ps[:])
+                nc.sync.dma_start(out[:, cols], o_sb[:])
+            else:
+                nc.scalar.copy(o_sb[:], o_ps[:])
+                nc.scalar.dma_start(out[:, cols], o_sb[:])

@@ -30,6 +30,7 @@ def tile_attend_answerodds_followed_read_kernel(
         lists = ctx.enter_context(tc.tile_pool(name="lists", bufs=1))
         sb = ctx.enter_context(tc.tile_pool(name="sb", bufs=1))
         late = ctx.enter_context(tc.tile_pool(name="late", bufs=1))
+        early = ctx.enter_context(tc.tile_pool(name="early", bufs=1))
         ps = ctx.enter_context(tc.psum_pool(name="ps", bufs=1))
 
         def bank(tag, name):
@@ -41,26 +42,30 @@ def tile_attend_answerodds_followed_read_kernel(
         warm = sb.tile([P, 8], F32, name="warm")
         warm_out = sb.tile([P, 8], F32, name="warm_out")
         nc.vector.memset(warm[:], 0.0)
+        ident = sb.tile([P, P], F32, name="ident")
+        nc.vector.memset(ident[:], 0.0)
+        make_identity(nc, ident[:], nomemset=True)
         ksc = sb.tile([P, T], U8, name="ksc", align_bytes=64)
-        nc.vector.memset(ksc[:].bitcast(I32), 0)
+        nc.gpsimd.memset(ksc[:].bitcast(I32), 0)
         thr_w = sb.tile([P, T], F32, name="thr_w", tag="row_a")
-        steep_w = sb.tile([P, T], F32, name="steep_w", tag="row_b")
+        steep_w = early.tile([P, T], F32, name="steep_w", offset=0, align_bytes=64)
         nc.vector.memset(thr_w[0:LIVE, :], 0.0)
-        nc.vector.memset(steep_w[0:LIVE, :], 0.0)
-        guess_w = sb.tile([P, T], F32, name="guess_w")
-        nc.vector.memset(guess_w[0:LIVE, 0:64], 0.0)
+        nc.gpsimd.memset(steep_w[0:LIVE, :], 0.0)
+        guess_w = sb.tile([P, T], F32, name="guess_w", tag="vg0")
+        one = sb.tile([P, 1], F32, name="one", tag="vg1")
+        nc.vector.memset(one[:], 1.0)
 
         nc.sync.dma_start(offs_sb[:], offs)
         nc.sync.dma_start(thr_w[LIVE:P, :], thr[0:1, :])
         nc.sync.dma_start(steep_w[LIVE:P, :], steep[0:1, :])
         nc.scalar.activation(warm_out[:], warm[:], ACT.Sigmoid)
+        q_raw = sb.tile([P, 4, Q], F32, name="q_raw", tag="q")
+        nc.sync.dma_start(q_raw[:], query.rearrange("(p j) q -> p j q", j=4))
         kw = sb.tile([P, T], I32, name="kw", align_bytes=64)
         nc.sync.dma_start(kw[:], keys_words[0].rearrange("p n t -> p (n t)").bitcast(I32))
         sc_rows = keys_scales[0].rearrange("(g r) n -> r g n", r=4)
         for r in range(4):
             nc.sync.dma_start(ksc[r:P:32, :].bitcast(I32), sc_rows[r].bitcast(I32))
-        q_raw = sb.tile([P, 4, Q], F32, name="q_raw", tag="q")
-        nc.sync.dma_start(q_raw[:], query.rearrange("(p j) q -> p j q", j=4))
         nc.sync.dma_start(guess_w[LIVE:P, :], guess[0:1, :])
         v_w = [sb.tile([P, T], F32, name="v_w%d" % j, tag="v%d" % j, align_bytes=64) for j in range(3)]
         v_w.append(late.tile([P, T], F32, name="v_w3", offset=0, align_bytes=64))
@@ -69,11 +74,9 @@ def tile_attend_answerodds_followed_read_kernel(
         nc.sync.dma_start(lam_sb[:], lam)
         nc.sync.dma_start(v_w[1][:], vals[P : 2 * P, :])
 
-        ident = sb.tile([P, P], F32, name="ident")
-        make_identity(nc, ident[:])
         r_w = sb.tile([P, R_WINDOW], F32, name="r_w")
+        nc.gpsimd.memset(guess_w[0:LIVE, :], 0.0)
         nc.gpsimd.memset(r_w[:, I:R_WINDOW], 0.0)
-        nc.gpsimd.memset(guess_w[0:LIVE, 32:T], 0.0)
 
         def turn4(dst, src):
             for t in range(4):
@@ -107,38 +110,41 @@ def tile_attend_answerodds_followed_read_kernel(
         for t in range(4):
             nc.scalar.activation(bias_c[:, t : t + 1], thr_t[:, t, LIVE:P], ACT.Copy, scale=nsteep_c[:, t : t + 1])
 
-        q_codes = sb.tile([P, Q], U32, name="q_codes", align_bytes=64)
+        q_codes = early.tile([P, Q], U32, name="q_codes", offset=2048, align_bytes=64)
         q_scales = sb.tile([P, Q], U8, name="q_scales", align_bytes=64)
 
-        kw_g = sb.tile([P, I], U32, name="kw_g", align_bytes=64)
+        kw_g = early.tile([P, I], U32, name="kw_g", offset=0, align_bytes=64)
         ksc_g = sb.tile([P, I], U8, name="ksc_g", align_bytes=64)
         nc.vector.tensor_copy(kw_g[:], kw[:].bitcast(U32).indirect(offs_sb[:]))
         nc.vector.quantize_mx(out=q_codes[:].bitcast(FP8X4), scales=q_scales[:], in_=q_bf[:].rearrange("p q j -> p (q j)"))
-        nc.vector.tensor_copy(ksc_g[:], ksc[:].indirect(offs_sb[:]))
-
-        a_t = bank("b3", "a_t")
-        for t in range(4):
-            cols = slice(t * P, (t + 1) * P)
-            nc.tensor.matmul_mx(
-                out=a_t[:, t, :],
-                lhsT=kw_g[:, cols].bitcast(FP8X4),
-                lhsT_scale=ksc_g[:, cols],
-                rhs=q_codes[:].bitcast(FP8X4),
-                rhs_scale=q_scales[:],
-                start=True,
-                stop=True,
-            )
         sg = sb.tile([P, 4, P], F32, name="sg")
-        for t in range(4):
-            nc.scalar.activation(sg[:, t, :], a_t[:, t, :], ACT.Sigmoid, bias=bias_c[:, t : t + 1], scale=steep_c[:, t : t + 1])
+        for h in range(2):
+            nc.vector.tensor_copy(ksc_g[:, h * 256 : (h + 1) * 256], ksc[:].indirect(offs_sb[:, h * 16 : (h + 1) * 16]))
+            a_t = ps.tile([P, 2, P], F32, tag="b%d" % (3 + h), name="a_t%d" % h)
+            for u in range(2):
+                cols = slice((2 * h + u) * P, (2 * h + u + 1) * P)
+                nc.tensor.matmul_mx(
+                    out=a_t[:, u, :],
+                    lhsT=kw_g[:, cols].bitcast(FP8X4),
+                    lhsT_scale=ksc_g[:, cols],
+                    rhs=q_codes[:].bitcast(FP8X4),
+                    rhs_scale=q_scales[:],
+                    start=True,
+                    stop=True,
+                )
+            for u in range(2):
+                t = 2 * h + u
+                nc.scalar.activation(sg[:, t, :], a_t[:, u, :], ACT.Sigmoid, bias=bias_c[:, t : t + 1], scale=steep_c[:, t : t + 1])
 
+        warm_ln = sb.tile([P, 1], F32, name="warm_ln")
+        nc.scalar.activation(warm_ln[:], sg[:, 3, 0:1], ACT.Ln, bias=1.0)
         guess_g = sb.tile([P, I], F32, name="guess_g")
         nc.vector.tensor_copy(guess_g[:], guess_w[:].indirect(offs_sb[:]))
         guess_t = bank("b2", "guess_t")
         turn4(guess_t, guess_g)
 
         def turn_values(j, v_t):
-            v_g = sb.tile([P, I], BF16, name="v_g%d" % j)
+            v_g = sb.tile([P, I], BF16, name="v_g%d" % j, tag="vg%d" % j)
             nc.vector.tensor_copy(v_g[:], v_w[j][:].indirect(offs_sb[:]))
             words = v_g[:].bitcast(F32)
             for u in range(2):
@@ -150,7 +156,7 @@ def tile_attend_answerodds_followed_read_kernel(
         guess_c = guess_rest[:, 0:4]
         rest_c = guess_rest[:, 4:8]
         nc.vector.tensor_copy(guess_c, guess_t[:, :, LIVE])
-        nc.vector.tensor_scalar(rest_c, guess_t[:, :, LIVE], -1.0, 1.0, ALU.mult, ALU.add)
+        nc.vector.tensor_scalar(rest_c, guess_t[:, :, LIVE], -1.0, one[:], ALU.mult, ALU.add)
         nlam = sb.tile([P, 1], F32, name="nlam")
         nc.gpsimd.tensor_scalar(nlam[:], lam_sb[:], -1.0, 0.0, ALU.mult, ALU.add)
 

@@ -46,14 +46,15 @@ def tile_attend_answerodds_followed_read_kernel(
         nc.vector.memset(ident[:], 0.0)
         make_identity(nc, ident[:], nomemset=True)
         ksc = sb.tile([P, T], U8, name="ksc", align_bytes=64)
-        nc.gpsimd.memset(ksc[:].bitcast(I32), 0)
         thr_w = sb.tile([P, T], F32, name="thr_w", tag="row_a")
         steep_w = early.tile([P, T], F32, name="steep_w", offset=0, align_bytes=64)
         nc.vector.memset(thr_w[0:LIVE, :], 0.0)
-        nc.gpsimd.memset(steep_w[0:LIVE, :], 0.0)
+        nc.vector.memset(steep_w[0:LIVE, :], 0.0)
+        nc.vector.memset(ksc[:].bitcast(I32), 0)
         guess_w = sb.tile([P, T], F32, name="guess_w", tag="vg0")
         one = sb.tile([P, 1], F32, name="one", tag="vg1")
-        nc.vector.memset(one[:], 1.0)
+        nc.vector.memset(guess_w[0:LIVE, 0:64], 0.0)
+        nc.gpsimd.memset(one[:], 1.0)
 
         nc.sync.dma_start(offs_sb[:], offs)
         nc.sync.dma_start(thr_w[LIVE:P, :], thr[0:1, :])
@@ -75,8 +76,8 @@ def tile_attend_answerodds_followed_read_kernel(
         nc.sync.dma_start(v_w[1][:], vals[P : 2 * P, :])
 
         r_w = sb.tile([P, R_WINDOW], F32, name="r_w")
-        nc.gpsimd.memset(guess_w[0:LIVE, :], 0.0)
         nc.gpsimd.memset(r_w[:, I:R_WINDOW], 0.0)
+        nc.gpsimd.memset(guess_w[0:LIVE, 32:T], 0.0)
 
         def turn4(dst, src):
             for t in range(4):
@@ -185,17 +186,19 @@ def tile_attend_answerodds_followed_read_kernel(
         nc.vector.tensor_scalar(r_w[:, 0:I], p_sb[:], inv_sum[:], None, ALU.mult)
         r_g = sb.tile([P, I], F32, name="r_g")
         nc.vector.tensor_copy(r_g[:], r_w[:].indirect(offs4_sb[:]))
-        w_d = sb.tile([P, I], F32, name="w_d")
-        nc.vector.scalar_tensor_tensor(
-            w_d[:].rearrange("p (t s) -> p s t", t=4),
-            r_g[:].rearrange("p (s t) -> p s t", t=4),
-            pull_sb[:],
-            r_w[:, 0:I].rearrange("p (s t) -> p s t", t=4),
-            ALU.mult,
-            ALU.add,
-        )
         w_t = bank("b1", "w_t")
-        turn4(w_t, w_d)
+        for u in range(2):
+            w_d = sb.tile([P, 2 * P], F32, name="w_d%d" % u)
+            nc.vector.scalar_tensor_tensor(
+                w_d[:].rearrange("p (s e) -> p s e", e=2),
+                r_g[:].rearrange("p (s t) -> p s t", t=4)[:, :, 2 * u : 2 * u + 2],
+                pull_sb[:],
+                r_w[:, 0:I].rearrange("p (s t) -> p s t", t=4)[:, :, 2 * u : 2 * u + 2],
+                ALU.mult,
+                ALU.add,
+            )
+            for e in range(2):
+                nc.tensor.transpose(w_t[:, 2 * u + e, :], w_d[:, e : 2 * P : 2], ident[:])
         v_t3 = ps.tile([P, 2, P], F32, tag="b0", name="v_t3")
         turn_values(3, v_t3)
         nc.scalar.copy(words23[:, 2 * P : 4 * P].rearrange("p (e u) -> p e u", u=2), v_t3[:].rearrange("p u e -> p e u"))

from contextlib import ExitStack

import concourse.mybir as mybir
from concourse.masks import make_identity

D, T, I, Q, E = 512, 2048, 512, 128, 512
FLOPS = 2 * Q * I * D + 2 * Q * I * E
BYTES = D * Q * 4 + D * T + 16 * T + 3 * T * 4 + 2 * Q * 4 + I * 4 + E * T * 4 + 2 * 128 * 32 * 2 + Q * E * 4

F32 = mybir.dt.float32
BF16 = mybir.dt.bfloat16
I32 = mybir.dt.int32
U32 = mybir.dt.uint32
U16 = mybir.dt.uint16
U8 = mybir.dt.uint8
FP8X4 = mybir.dt.float8_e4m3fn_x4
ALU = mybir.AluOpType
ACT = mybir.ActivationFunctionType

P = 128
LIVE = P - 1
R_WINDOW = 704


def tile_attend_answerodds_followed_read_kernel(
    tc, query, keys_words, keys_scales, guess, steep, thr, lam, pull, slot_factor, vals, offs, offs4, out
):
    nc = tc.nc
    with ExitStack() as ctx:
        lists = ctx.enter_context(tc.tile_pool(name="lists", bufs=1))
        sb = ctx.enter_context(tc.tile_pool(name="sb", bufs=1))
        late = ctx.enter_context(tc.tile_pool(name="late", bufs=1))
        early = ctx.enter_context(tc.tile_pool(name="early", bufs=1))
        ps = ctx.enter_context(tc.psum_pool(name="ps", bufs=1))

        def bank(tag, name):
            return ps.tile([P, 4, P], F32, tag=tag, name=name)

        offs_sb = lists.tile([P, I // 16], U16, name="offs_sb")
        offs4_sb = lists.tile([P, I // 16], U16, name="offs4_sb")

        warm = sb.tile([P, 8], F32, name="warm")
        warm_out = sb.tile([P, 8], F32, name="warm_out")
        nc.vector.memset(warm[:], 0.0)
        ident = sb.tile([P, P], F32, name="ident")
        nc.vector.memset(ident[:], 0.0)
        make_identity(nc, ident[:], nomemset=True)
        ksc = sb.tile([P, T], U8, name="ksc", align_bytes=64)
        thr_w = sb.tile([P, T], F32, name="thr_w", tag="row_a")
        steep_w = early.tile([P, T], F32, name="steep_w", offset=0, align_bytes=64)
        nc.vector.memset(thr_w[0:LIVE, :], 0.0)
        nc.vector.memset(steep_w[0:LIVE, :], 0.0)
        nc.vector.memset(ksc[:].bitcast(I32), 0)
        guess_w = sb.tile([P, T], F32, name="guess_w", tag="vg0")
        one = sb.tile([P, 1], F32, name="one", tag="vg1")
        nc.vector.memset(guess_w[0:LIVE, 0:64], 0.0)
        nc.gpsimd.memset(one[:], 1.0)

        nc.sync.dma_start(offs_sb[:], offs)
        nc.sync.dma_start(thr_w[LIVE:P, :], thr[0:1, :])
        nc.sync.dma_start(steep_w[LIVE:P, :], steep[0:1, :])
        nc.scalar.activation(warm_out[:], warm[:], ACT.Sigmoid)
        q_raw = sb.tile([P, 4, Q], F32, name="q_raw", tag="q")
        nc.sync.dma_start(q_raw[:], query.rearrange("(p j) q -> p j q", j=4))
        kw = sb.tile([P, T], I32, name="kw", align_bytes=64)
        nc.sync.dma_start(kw[:], keys_words[0].rearrange("p n t -> p (n t)").bitcast(I32))
        sc_rows = keys_scales[0].rearrange("(g r) n -> r g n", r=4)
        for r in range(4):
            nc.sync.dma_start(ksc[r:P:32, :].bitcast(I32), sc_rows[r].bitcast(I32))
        nc.sync.dma_start(guess_w[LIVE:P, :], guess[0:1, :])
        v_w = [sb.tile([P, T], F32, name="v_w%d" % j, tag="v%d" % j, align_bytes=64) for j in range(3)]
        v_w.append(late.tile([P, T], F32, name="v_w3", offset=0, align_bytes=64))
        nc.sync.dma_start(v_w[0][:], vals[0:P, :])
        lam_sb = sb.tile([P, 1], F32, name="lam_sb")
        nc.sync.dma_start(lam_sb[:], lam)
        nc.sync.dma_start(v_w[1][:], vals[P : 2 * P, :])

        r_w = sb.tile([P, R_WINDOW], F32, name="r_w")
        nc.gpsimd.memset(r_w[:, I:R_WINDOW], 0.0)
        nc.gpsimd.memset(guess_w[0:LIVE, 32:T], 0.0)

        def turn4(dst, src):
            for t in range(4):
                nc.tensor.transpose(dst[:, t, :], src[:, t * P : (t + 1) * P], ident[:])

        thr_g = sb.tile([P, I], F32, name="thr_g")
        nc.vector.tensor_copy(thr_g[:], thr_w[:].indirect(offs_sb[:]))
        steep_g = sb.tile([P, I], F32, name="steep_g")
        nc.vector.tensor_copy(steep_g[:], steep_w[:].indirect(offs_sb[:]))
        thr_t = bank("b0", "thr_t")
        turn4(thr_t, thr_g)
        steep_t = bank("b1", "steep_t")
        turn4(steep_t, steep_g)

        nc.sync.dma_start(offs4_sb[:], offs4)
        pull_sb = sb.tile([P, 1], F32, name="pull_sb")
        nc.sync.dma_start(pull_sb[:], pull)
        os_sb = sb.tile([P, 4], F32, name="os_sb")
        nc.sync.dma_start(os_sb[:], slot_factor.rearrange("o (p t) -> (o p) t", t=4))
        for j in range(2, 4):
            nc.sync.dma_start(v_w[j][:], vals[j * P : (j + 1) * P, :])

        q_bf = sb.tile([P, Q, 4], BF16, name="q_bf", align_bytes=64)
        nc.scalar.copy(q_bf[:], q_raw[:].rearrange("p j q -> p q j"))
        steep_pair = sb.tile([P, 8], F32, name="steep_pair", tag="q")
        steep_c = steep_pair[:, 0:4]
        nsteep_c = steep_pair[:, 4:8]
        bias_c = sb.tile([P, 4], F32, name="bias_c")
        nc.scalar.activation(steep_c, steep_t[:, :, LIVE], ACT.Copy)
        nc.scalar.activation(nsteep_c, steep_t[:, :, LIVE], ACT.Copy, scale=-1.0)
        for t in range(4):
            nc.scalar.activation(bias_c[:, t : t + 1], thr_t[:, t, LIVE:P], ACT.Copy, scale=nsteep_c[:, t : t + 1])

        q_codes = early.tile([P, Q], U32, name="q_codes", offset=2048, align_bytes=64)
        q_scales = sb.tile([P, Q], U8, name="q_scales", align_bytes=64)

        kw_g = early.tile([P, I], U32, name="kw_g", offset=0, align_bytes=64)
        ksc_g = sb.tile([P, I], U8, name="ksc_g", align_bytes=64)
        nc.vector.tensor_copy(kw_g[:], kw[:].bitcast(U32).indirect(offs_sb[:]))
        nc.vector.quantize_mx(out=q_codes[:].bitcast(FP8X4), scales=q_scales[:], in_=q_bf[:].rearrange("p q j -> p (q j)"))
        sg = sb.tile([P, 4, P], F32, name="sg")
        for h in range(2):
            nc.vector.tensor_copy(ksc_g[:, h * 256 : (h + 1) * 256], ksc[:].indirect(offs_sb[:, h * 16 : (h + 1) * 16]))
            a_t = ps.tile([P, 2, P], F32, tag="b%d" % (3 + h), name="a_t%d" % h)
            for u in range(2):
                cols = slice((2 * h + u) * P, (2 * h + u + 1) * P)
                nc.tensor.matmul_mx(
                    out=a_t[:, u, :],
                    lhsT=kw_g[:, cols].bitcast(FP8X4),
                    lhsT_scale=ksc_g[:, cols],
                    rhs=q_codes[:].bitcast(FP8X4),
                    rhs_scale=q_scales[:],
                    start=True,
                    stop=True,
                )
            for u in range(2):
                t = 2 * h + u
                nc.scalar.activation(sg[:, t, :], a_t[:, u, :], ACT.Sigmoid, bias=bias_c[:, t : t + 1], scale=steep_c[:, t : t + 1])

        warm_ln = sb.tile([P, 1], F32, name="warm_ln")
        nc.scalar.activation(warm_ln[:], sg[:, 3, 0:1], ACT.Ln, bias=1.0)
        guess_g = sb.tile([P, I], F32, name="guess_g")
        nc.vector.tensor_copy(guess_g[:], guess_w[:].indirect(offs_sb[:]))
        guess_t = bank("b2", "guess_t")
        turn4(guess_t, guess_g)

        def turn_values(j, v_t):
            v_g = sb.tile([P, I], BF16, name="v_g%d" % j, tag="vg%d" % j)
            nc.vector.tensor_copy(v_g[:], v_w[j][:].indirect(offs_sb[:]))
            words = v_g[:].bitcast(F32)
            for u in range(2):
                nc.tensor.transpose(v_t[:, u, :], words[:, u : 2 * P : 2], ident[:])

        v_t01 = ps.tile([P, 2, 2, P], F32, tag="bv0", name="v_t01")
        turn_values(0, v_t01[:, 0, :, :])
        guess_rest = sb.tile([P, 8], F32, name="guess_rest", tag="v0", align_bytes=64)
        guess_c = guess_rest[:, 0:4]
        rest_c = guess_rest[:, 4:8]
        nc.vector.tensor_copy(guess_c, guess_t[:, :, LIVE])
        nc.vector.tensor_scalar(rest_c, guess_t[:, :, LIVE], -1.0, one[:], ALU.mult, ALU.add)
        nlam = sb.tile([P, 1], F32, name="nlam")
        nc.gpsimd.tensor_scalar(nlam[:], lam_sb[:], -1.0, 0.0, ALU.mult, ALU.add)

        ln_t = sb.tile([P, I], F32, name="ln_t")
        for t in range(4):
            nc.scalar.activation(ln_t[:, t * P : (t + 1) * P], sg[:, t, :], ACT.Ln, bias=guess_c[:, t : t + 1], scale=rest_c[:, t : t + 1])
        turn_values(1, v_t01[:, 1, :, :])
        ln_q = bank("b0", "ln_q")
        turn4(ln_q, ln_t)
        neg_s = sb.tile([P, I], F32, name="neg_s", tag="v1", align_bytes=64)
        neg_max = sb.tile([P, 1], F32, name="neg_max")
        nc.vector.tensor_scalar(neg_s[:], ln_q[:].rearrange("p t s -> p (t s)"), nlam[:], None, ALU.mult, ALU.min, accum_out=neg_max[:])
        v_t2 = ps.tile([P, 2, P], F32, tag="bv1", name="v_t2")
        turn_values(2, v_t2)
        p_sb = sb.tile([P, I], F32, name="p_sb")
        row_sum = sb.tile([P, 1], F32, name="row_sum")
        nc.scalar.activation(p_sb[:], neg_s[:], ACT.Exp, bias=neg_max[:], scale=-1.0, accum_out=row_sum[:])
        v_bf01 = sb.tile([P, 2 * P, 4], BF16, name="v_bf01", tag="v1", align_bytes=64)
        v_bf23 = sb.tile([P, 2 * P, 4], BF16, name="v_bf23", align_bytes=64)
        words01 = v_bf01[:].rearrange("p e t -> p (e t)").bitcast(F32)
        words23 = v_bf23[:].rearrange("p e t -> p (e t)").bitcast(F32)
        nc.scalar.copy(words01.rearrange("p (j e u) -> p j e u", j=2, u=2), v_t01[:].rearrange("p j u e -> p j e u"))
        nc.scalar.copy(words23[:, 0 : 2 * P].rearrange("p (e u) -> p e u", u=2), v_t2[:].rearrange("p u e -> p e u"))
        inv_sum = sb.tile([P, 1], F32, name="inv_sum", tag="v2", align_bytes=64)
        nc.vector.reciprocal(inv_sum[:], row_sum[:])
        nc.vector.tensor_scalar(r_w[:, 0:I], p_sb[:], inv_sum[:], None, ALU.mult)
        r_g = sb.tile([P, I], F32, name="r_g")
        nc.vector.tensor_copy(r_g[:], r_w[:].indirect(offs4_sb[:]))
        w_t = bank("b1", "w_t")
        for u in range(2):
            w_d = sb.tile([P, 2 * P], F32, name="w_d%d" % u)
            nc.vector.scalar_tensor_tensor(
                w_d[:].rearrange("p (s e) -> p s e", e=2),
                r_g[:].rearrange("p (s t) -> p s t", t=4)[:, :, 2 * u : 2 * u + 2],
                pull_sb[:],
                r_w[:, 0:I].rearrange("p (s t) -> p s t", t=4)[:, :, 2 * u : 2 * u + 2],
                ALU.mult,
                ALU.add,
            )
            for e in range(2):
                nc.tensor.transpose(w_t[:, 2 * u + e, :], w_d[:, e : 2 * P : 2], ident[:])
        v_t3 = ps.tile([P, 2, P], F32, tag="b0", name="v_t3")
        turn_values(3, v_t3)
        nc.scalar.copy(words23[:, 2 * P : 4 * P].rearrange("p (e u) -> p e u", u=2), v_t3[:].rearrange("p u e -> p e u"))
        w_bf = late.tile([P, Q, 4], BF16, name="w_bf", offset=0, align_bytes=64)
        nc.vector.tensor_tensor(w_bf[:], w_t[:].rearrange("p t q -> p q t"), os_sb[:].unsqueeze(1).to_broadcast([P, Q, 4]), ALU.mult)
        half = E // 2
        v_codes = [late.tile([P, half], U32, name="v_codes%d" % h, offset=1024 * (1 + h), align_bytes=64) for h in range(2)]
        v_scales = [sb.tile([P, half], U8, name="v_scales%d" % h, align_bytes=64) for h in range(2)]
        nc.vector.quantize_mx(out=v_codes[0][:].bitcast(FP8X4), scales=v_scales[0][:], in_=v_bf01[:].rearrange("p e t -> p (e t)"))
        w_codes = sb.tile([P, Q], U32, name="w_codes", align_bytes=64)
        w_scales = sb.tile([P, Q], U8, name="w_scales", align_bytes=64)
        nc.vector.quantize_mx(out=w_codes[:].bitcast(FP8X4), scales=w_scales[:], in_=w_bf[:].rearrange("p q t -> p (q t)"))
        nc.vector.quantize_mx(out=v_codes[1][:].bitcast(FP8X4), scales=v_scales[1][:], in_=v_bf23[:].rearrange("p e t -> p (e t)"))

        for h in range(2):
            cols = slice(h * half, (h + 1) * half)
            o_ps = ps.tile([P, half], F32, tag="b%d" % (2 + h), name="o_ps%d" % h)
            nc.tensor.matmul_mx(
                out=o_ps[:],
                lhsT=w_codes[:].bitcast(FP8X4),
                lhsT_scale=w_scales[:],
                rhs=v_codes[h][:].bitcast(FP8X4),
                rhs_scale=v_scales[h][:],
                start=True,
                stop=True,
            )
            o_sb = sb.tile([P, half], F32, name="o_sb%d" % h)
            if h == 1:
                nc.vector.tensor_copy(o_sb[:], o_ps[:])
                nc.sync.dma_start(out[:, cols], o_sb[:])
            else:
                nc.scalar.copy(o_sb[:], o_ps[:])
                nc.scalar.dma_start(out[:, cols], o_sb[:])
